import numpy as np
import ml_dtypes


def mxq(x, axis, fmt="e4m3"):
    dtype, down = {"e4m3": (ml_dtypes.float8_e4m3fn, 7), "e5m2": (ml_dtypes.float8_e5m2, 14)}[fmt]
    v = np.moveaxis(np.asarray(x, np.float32).astype(ml_dtypes.bfloat16).astype(np.float64), axis, -1)
    blocks = v.reshape(v.shape[:-1] + (-1, 32))
    amax = np.abs(blocks).max(-1, keepdims=True)
    byte = np.maximum(np.where(amax > 0, np.frexp(amax)[1] - 1 + 127, 0) - down, 1)
    scale = np.exp2(byte - 127.0)
    codes = (blocks / scale).astype(np.float32).astype(dtype).astype(np.float64)
    return np.moveaxis((codes * scale).reshape(v.shape), -1, axis)


WIDE = False


def mx_kscale(k):
    if not WIDE:
        return np.ones(k)
    levels = np.array([10, -10, 5, -5, 0])
    if k % 512:
        return np.exp2(np.random.permutation(np.resize(levels, k // 32))).repeat(32)
    a = np.empty((k // 512, 16))
    for p in range(k // 512):
        a[p, :8] = np.random.permutation(np.resize(levels, 8))
        for g in range(8):
            far = levels[np.abs(levels - a[p, g]) >= 10]
            a[p, g + 8] = far[np.random.randint(len(far))]
    return np.exp2(a.ravel()).repeat(32)


def f64(x):
    return np.asarray(x).astype(np.float64)


E2M1 = np.array([0.0, 0.5, 1.0, 1.5, 2.0, 3.0, 4.0, 6.0, -0.0, -0.5, -1.0, -1.5, -2.0, -3.0, -4.0, -6.0])


def pack_weight(w, fmt):
    k, n = w.shape
    w = f64(np.asarray(w, np.float32).astype(ml_dtypes.bfloat16)).reshape(k // 32, 32, n)
    amax = np.abs(w).max(1)
    if fmt == "e4m3":
        byte = np.frexp(amax)[1] - 1 + 127 - 7
    else:
        mant, ex = np.frexp(amax / 6.0)
        byte = np.where(mant > 0.5, ex, ex - 1) + 127
    byte = np.clip(np.where(amax > 0, byte, 1), 1, 254)
    scaled = (w * np.exp2(127.0 - byte)[:, None, :]).reshape(k, n).astype(np.float32)
    by_word = np.ascontiguousarray(scaled.reshape(k // 512, 128, 4, n).transpose(0, 1, 3, 2))
    if fmt == "e4m3":
        words = by_word.astype(ml_dtypes.float8_e4m3fn).view(np.uint8)
    else:
        c = by_word.astype(ml_dtypes.float4_e2m1fn).view(np.uint8) & 0xF
        words = (c[..., 0::2] | (c[..., 1::2] << 4)).reshape(k // 512, 128, 2 * n)
    return np.ascontiguousarray(words), np.ascontiguousarray(byte.astype(np.uint8).reshape(k // 512, 16, n))


def unpack_weight(words, scales, fmt):
    g, _, n = scales.shape
    words = np.ascontiguousarray(words).reshape(g, 128, n, -1)
    if fmt == "e4m3":
        vals = words.view(ml_dtypes.float8_e4m3fn).astype(np.float64)
    else:
        nib = np.empty((g, 128, n, 4), np.uint8)
        nib[..., 0::2] = words & 0xF
        nib[..., 1::2] = words >> 4
        vals = E2M1[nib]
    vals = vals * np.repeat(np.exp2(scales.astype(np.float64) - 127.0), 8, axis=1)[..., None]
    return vals.transpose(0, 1, 3, 2).reshape(g * 512, n)


def bf(x):
    return np.asarray(x, np.float32).astype(ml_dtypes.bfloat16)


def planes(Y):
    r, m = Y.shape
    b = f64(bf(Y)).reshape(r // 32, 32, m)
    amax = np.abs(b).max(1)
    byte = np.clip(np.where(amax > 0, np.frexp(amax)[1] - 1 + 127 - 7, 1), 1, 254)
    codes = (b * np.exp2(127.0 - byte)[:, None, :]).reshape(r, m).astype(np.float32).astype(ml_dtypes.float8_e4m3fn).view(np.uint8)
    words = codes.reshape(r // 512, 128, 4, m).transpose(0, 1, 3, 2)
    return np.ascontiguousarray(words), np.ascontiguousarray(byte.astype(np.uint8).reshape(r // 512, 16, m))


K, L, T, R, N = 1024, 512, 512, 512, 512


def setup_inputs():
    n = np.random.standard_normal
    fk = mx_kscale(K)
    fl = mx_kscale(L)
    fr = mx_kscale(R)
    xtp = pack_weight(n((K, T)) / fk[:, None], "e2m1")
    wap = pack_weight(n((K, R)) * 1.4 / np.sqrt(K) * fk[:, None], "e4m3")
    xqp = pack_weight(n((L, T)) / fl[:, None], "e2m1")
    wcp = pack_weight(n((L, R)) * 1 / np.sqrt(L) * fl[:, None], "e4m3")
    wbp = pack_weight(n((R, N)) * 1 / np.sqrt(R) / fr[:, None], "e2m1")
    wdp = pack_weight(n((R, N)) * 1 / np.sqrt(R) / fr[:, None], "e4m3")
    return {
        "xt_words": xtp[0],
        "xt_scales": xtp[1],
        "wa_words": wap[0],
        "wa_scales": wap[1],
        "xq_words": xqp[0],
        "xq_scales": xqp[1],
        "wc_words": wcp[0],
        "wc_scales": wcp[1],
        "us": (np.random.uniform(0.5, 2.0, (R, 1)) * fr[:, None]).astype(np.float32),
        "ur": (np.random.uniform(0.5, 2.0, (R, 1)) * fr[:, None]).astype(np.float32),
        "wb_words": wbp[0],
        "wb_scales": wbp[1],
        "wd_words": wdp[0],
        "wd_scales": wdp[1],
    }


def reference(xt_words, xt_scales, wa_words, wa_scales, xq_words, xq_scales, wc_words, wc_scales, us, ur, wb_words, wb_scales, wd_words, wd_scales):
    xtu = unpack_weight(xt_words, xt_scales, "e2m1")
    wau = unpack_weight(wa_words, wa_scales, "e4m3")
    xqu = unpack_weight(xq_words, xq_scales, "e2m1")
    wcu = unpack_weight(wc_words, wc_scales, "e4m3")
    wbu = unpack_weight(wb_words, wb_scales, "e2m1")
    wdu = unpack_weight(wd_words, wd_scales, "e4m3")
    z = wau.T @ xtu + wcu.T @ xqu
    kp = np.maximum(np.minimum(z, 1.0), 0.0 - 1.0)
    ha = kp * f64(us)
    hb = (z - kp) * f64(ur)
    haq = mxq(ha, 0, "e4m3")
    hbq = mxq(hb, 0, "e4m3")
    y = wbu.T @ haq + wdu.T @ hbq
    words, scales = planes(y)
    return y, words, scales

@@ -1,0 +1,232 @@
+from contextlib import ExitStack
+
+import concourse.mybir as mybir
+
+K, L, T, R, N = 1024, 512, 512, 512, 512
+FLOPS = 2 * T * (K * R + L * R + 2 * R * N)
+
+F32 = mybir.dt.float32
+BF16 = mybir.dt.bfloat16
+I32 = mybir.dt.int32
+U8 = mybir.dt.uint8
+FP8X4 = mybir.dt.float8_e4m3fn_x4
+FP4X4 = mybir.dt.float4_e2m1fn_x4
+ALU = mybir.AluOpType
+ACT = mybir.ActivationFunctionType
+
+P = 128
+PACK = 4
+QUADS = 4
+TC = 128
+CHUNKS = T // TC
+RUN = 4
+
+
+def tile_mix_hidden_kept_and_cut_off_pl_kernel(
+    tc, xt_words, xt_scales, wa_words, wa_scales, xq_words, xq_scales, wc_words, wc_scales,
+    us, ur, wb_words, wb_scales, wd_words, wd_scales, out_0, out_1, out_2,
+):
+    nc = tc.nc
+    with ExitStack() as ctx:
+        sb = ctx.enter_context(tc.tile_pool(name="sb", bufs=1))
+        ps = ctx.enter_context(tc.psum_pool(name="ps", bufs=1))
+        ctx.enter_context(tc.manual_schedule())
+
+        def tile(name, shape, dtype):
+            return sb.tile(shape, dtype, name=name, align_bytes=64)
+
+        def load_fp8(queue, name, words):
+            passes = words.shape[0]
+            raw = tile(name, [P, passes, words.shape[2]], I32)
+            queue.dma_start(out=raw[:], in_=words.rearrange("z p c b -> p z (c b)").bitcast(I32))
+            return raw
+
+        def load_fp4(queue, name, words):
+            passes = words.shape[0]
+            raw = tile(name, [P, passes, words.shape[2]], U8)
+            queue.dma_start(out=raw[:].bitcast(I32), in_=words.rearrange("z p c -> p z c").bitcast(I32))
+            return raw
+
+        def zeroed_plane(name, passes, engine=nc.vector):
+            plane = tile(name, [P, passes, T], U8)
+            engine.memset(plane[:].bitcast(I32), 0)
+            return plane
+
+        def load_scale_rows(queue, plane, scales, quad, first_row=0):
+            lo = 32 * quad + first_row
+            queue.dma_start(
+                out=plane[:].bitcast(I32)[lo : lo + 4],
+                in_=scales[:, 4 * quad : 4 * quad + 4, :].rearrange("z r c -> r z c").bitcast(I32),
+            )
+
+        def deal(name, raw, dtype):
+            passes, width = raw.shape[1], raw.shape[2]
+            dealt = tile(name, [P, passes, width], dtype)
+            b = width // (PACK * P)
+            if b == 1:
+                nc.vector.tensor_copy(
+                    out=dealt[:].rearrange("p z (j m) -> p z j m", j=PACK),
+                    in_=raw[:].rearrange("p z (m j) -> p z j m", j=PACK),
+                )
+            else:
+                nc.vector.tensor_copy(
+                    out=dealt[:, 0, :].rearrange("p (j m b) -> p j m b", j=PACK, b=b),
+                    in_=raw[:, 0, :].rearrange("p (m j b) -> p j m b", j=PACK, b=b),
+                )
+            return dealt
+
+        wa_s_raw = zeroed_plane("wa_s_raw", 2)
+        xt_s = zeroed_plane("xt_s", 2)
+        xq_s = zeroed_plane("xq_s", 1)
+        wc_s_raw = zeroed_plane("wc_s_raw", 1)
+        w2_s_raw = zeroed_plane("w2_s_raw", 1, nc.gpsimd)
+        warm = tile("warm", [P, 2], F32)
+        nc.vector.memset(warm[:, 0:1], 0.0)
+
+        wa_raw = load_fp8(nc.sync, "wa_raw", wa_words)
+        xt_w = load_fp4(nc.sync, "xt_w", xt_words)
+        for q in range(QUADS):
+            load_scale_rows(nc.scalar, wa_s_raw, wa_scales, q)
+        nc.scalar.activation(out=warm[:, 1:2], in_=warm[:, 0:1], func=ACT.Copy)
+        for q in range(QUADS):
+            load_scale_rows(nc.sync, xt_s, xt_scales, q)
+        for q in range(QUADS):
+            load_scale_rows(nc.gpsimd, w2_s_raw, wd_scales, q, first_row=4)
+        wc_raw = load_fp8(nc.sync, "wc_raw", wc_words)
+        xq_w = load_fp4(nc.sync, "xq_w", xq_words)
+        for q in range(QUADS):
+            load_scale_rows(nc.sync, wc_s_raw, wc_scales, q)
+        for q in range(QUADS):
+            load_scale_rows(nc.sync, xq_s, xq_scales, q)
+        factor = tile("factor", [P, 2, 8], F32)
+        for h, vec in enumerate((us, ur)):
+            nc.sync.dma_start(out=factor[:, h, 0:PACK], in_=vec.rearrange("(p j) o -> p (j o)", j=PACK))
+        wb_raw = load_fp4(nc.sync, "wb_raw", wb_words)
+        wd_raw = load_fp8(nc.sync, "wd_raw", wd_words)
+        for q in range(QUADS):
+            load_scale_rows(nc.sync, w2_s_raw, wb_scales, q)
+
+        wa_s = deal("wa_s", wa_s_raw, U8)
+        wa_w = deal("wa_w", wa_raw, I32)
+        wc_w = deal("wc_w", wc_raw, I32)
+        wc_s = deal("wc_s", wc_s_raw, U8)
+
+        upper = tile("upper", [P, 2, PACK], F32)
+        lower = tile("lower", [P, 2, PACK], F32)
+        nc.scalar.activation(out=upper[:], in_=factor[:, :, 0:PACK], func=ACT.Abs)
+        nc.scalar.activation(out=lower[:], in_=upper[:], func=ACT.Copy, scale=-1.0)
+
+        z = [ps.tile([P, PACK, TC], F32, name="z%d" % c) for c in range(CHUNKS)]
+        y = [ps.tile([P, PACK, TC], F32, name="y%d" % c) for c in range(CHUNKS)]
+        first = [(wa_w, wa_s, xt_w, xt_s, 0), (wa_w, wa_s, xt_w, xt_s, 1), (wc_w, wc_s, xq_w, xq_s, 0)]
+        for c in range(CHUNKS):
+            for n, (w, w_s, x, x_s, g) in enumerate(first):
+                for j in range(PACK):
+                    nc.tensor.matmul_mx(
+                        out=z[c][:, j, :],
+                        lhsT=w[:, g, P * j : P * (j + 1)].bitcast(FP8X4),
+                        lhsT_scale=w_s[:, g, P * j : P * (j + 1)],
+                        rhs=x[:, g, 2 * TC * c : 2 * TC * (c + 1)].bitcast(FP4X4),
+                        rhs_scale=x_s[:, g, TC * c : TC * (c + 1)],
+                        start=(n == 0 and j == 0),
+                        stop=(n == len(first) - 1 and j == PACK - 1),
+                    )
+
+        scaled = [tile("scaled%d" % c, [P, 2, PACK, TC], F32) for c in range(CHUNKS)]
+        kept_a = [tile("kept_a%d" % c, [P, PACK, TC], BF16) for c in range(CHUNKS)]
+        kept_b = [tile("kept_b%d" % c, [P, PACK, TC], F32) for c in range(CHUNKS)]
+        h16 = [tile("h16_%d" % c, [P, 2, TC * PACK], BF16) for c in range(CHUNKS)]
+        h_w = [tile("h_w%d" % c, [P, 2 * TC], I32) for c in range(CHUNKS)]
+        h_s = [tile("h_s%d" % c, [P, 2 * TC], U8) for c in range(CHUNKS)]
+        y16 = [tile("y16_%d" % c, [P, TC, PACK], BF16) for c in range(CHUNKS)]
+        y32 = [tile("y32_%d" % c, [P, PACK, TC], F32) for c in range(CHUNKS)]
+        y_w = [tile("y_w%d" % c, [P, TC], I32) for c in range(CHUNKS)]
+        y_s = tile("y_s", [P, T], U8)
+
+        def scale_z(c):
+            for h in range(2):
+                for j in range(PACK):
+                    nc.scalar.activation(
+                        out=scaled[c][:, h, j, :], in_=z[c][:, j, :], func=ACT.Copy, scale=factor[:, h, j : j + 1]
+                    )
+
+        def clip(c):
+            for h, kept in enumerate((kept_a, kept_b)):
+                for j in range(PACK):
+                    nc.vector.tensor_scalar(
+                        out=kept[c][:, j, :], in0=scaled[c][:, h, j, :],
+                        scalar1=upper[:, h, j : j + 1], scalar2=lower[:, h, j : j + 1],
+                        op0=ALU.min, op1=ALU.max,
+                    )
+
+        def by_word(region):
+            return region.rearrange("p j (u i) -> p u j i", i=RUN)
+
+        def interleave(c):
+            for_quant = [h16[c][:, h, :].rearrange("p (u i j) -> p u j i", i=RUN, j=PACK) for h in range(2)]
+            nc.vector.tensor_copy(out=for_quant[0], in_=by_word(kept_a[c][:]))
+            nc.vector.tensor_tensor(
+                out=for_quant[1], in0=by_word(scaled[c][:, 1]), in1=by_word(kept_b[c][:]), op=ALU.subtract
+            )
+
+        def quantise_h(c):
+            nc.vector.quantize_mx(
+                out=h_w[c][:].bitcast(FP8X4), scales=h_s[c][:], in_=h16[c][:].rearrange("p h w -> p (h w)")
+            )
+
+        def second_layer(c, wb_w, wd_w, w2_s):
+            for i in range(PACK):
+                nc.tensor.matmul_mx(
+                    out=y[c][:, i, :],
+                    lhsT=wb_w[:, 0, 2 * P * i : 2 * P * (i + 1)].bitcast(FP4X4),
+                    lhsT_scale=w2_s[:, 0, P * i : P * (i + 1)],
+                    rhs=h_w[c][:, 0:TC].bitcast(FP8X4), rhs_scale=h_s[c][:, 0:TC],
+                    start=True, stop=False,
+                )
+                nc.tensor.matmul_mx(
+                    out=y[c][:, i, :],
+                    lhsT=wd_w[:, 0, P * i : P * (i + 1)].bitcast(FP8X4),
+                    lhsT_scale=w2_s[4:P, 0, P * i : P * (i + 1)],
+                    rhs=h_w[c][:, TC : 2 * TC].bitcast(FP8X4), rhs_scale=h_s[c][:, TC : 2 * TC],
+                    start=False, stop=True,
+                )
+
+        out_rows = out_0.rearrange("(p i) t -> p i t", i=PACK)
+        out_words = out_1.rearrange("z p c b -> p (z c b)").bitcast(I32)
+
+        def drain_y(c):
+            nc.scalar.copy(out=y16[c][:], in_=y[c][:].rearrange("p i t -> p t i"))
+            nc.scalar.copy(out=y32[c][:], in_=y[c][:])
+            nc.sync.dma_start(out=out_rows[:, :, TC * c : TC * (c + 1)], in_=y32[c][:])
+
+        def quantise_y(c):
+            nc.vector.quantize_mx(
+                out=y_w[c][:].bitcast(FP8X4), scales=y_s[:, TC * c : TC * (c + 1)],
+                in_=y16[c][:].rearrange("p t i -> p (t i)"),
+            )
+            nc.sync.dma_start(out=out_words[:, TC * c : TC * (c + 1)], in_=y_w[c][:])
+
+        for c in range(CHUNKS):
+            scale_z(c)
+        clip(0)
+        interleave(0)
+        wb_w = deal("wb_w", wb_raw, U8)
+        wd_w = deal("wd_w", wd_raw, I32)
+        quantise_h(0)
+        w2_s = deal("w2_s", w2_s_raw, U8)
+        second_layer(0, wb_w, wd_w, w2_s)
+        drain_y(0)
+        for c in range(1, CHUNKS):
+            clip(c)
+            interleave(c)
+            quantise_y(c - 1)
+            quantise_h(c)
+            second_layer(c, wb_w, wd_w, w2_s)
+            drain_y(c)
+        quantise_y(CHUNKS - 1)
+        for q in range(QUADS):
+            queue = nc.sync if q % 2 == 0 else nc.scalar
+            queue.dma_start(
+                out=out_2[0, 4 * q : 4 * q + 4, :].bitcast(I32),
+                in_=y_s[:].bitcast(I32)[32 * q : 32 * q + 4],
+            )

@@ -19,7 +19,6 @@ PACK = 4
 QUADS = 4
 TC = 128
 CHUNKS = T // TC
-RUN = 4
 
 
 def tile_mix_hidden_kept_and_cut_off_pl_kernel(
@@ -64,9 +63,10 @@ def tile_mix_hidden_kept_and_cut_off_pl_kernel(
             dealt = tile(name, [P, passes, width], dtype)
             b = width // (PACK * P)
             if b == 1:
+                pair = 2 if dtype == I32 else P
                 nc.vector.tensor_copy(
-                    out=dealt[:].rearrange("p z (j m) -> p z j m", j=PACK),
-                    in_=raw[:].rearrange("p z (m j) -> p z j m", j=PACK),
+                    out=dealt[:].rearrange("p z (j u i) -> p z u j i", j=PACK, i=pair),
+                    in_=raw[:].rearrange("p z (u i j) -> p z u j i", j=PACK, i=pair),
                 )
             else:
                 nc.vector.tensor_copy(
@@ -75,40 +75,36 @@ def tile_mix_hidden_kept_and_cut_off_pl_kernel(
                 )
             return dealt
 
+        xq_s = zeroed_plane("xq_s", 1, nc.gpsimd)
+        for q in range(QUADS):
+            load_scale_rows(nc.gpsimd, xq_s, xq_scales, q)
         wa_s_raw = zeroed_plane("wa_s_raw", 2)
         xt_s = zeroed_plane("xt_s", 2)
-        xq_s = zeroed_plane("xq_s", 1)
         wc_s_raw = zeroed_plane("wc_s_raw", 1)
-        w2_s_raw = zeroed_plane("w2_s_raw", 1, nc.gpsimd)
+        w2_s_raw = zeroed_plane("w2_s_raw", 1)
         warm = tile("warm", [P, 2], F32)
         nc.vector.memset(warm[:, 0:1], 0.0)
+        nc.scalar.activation(out=warm[:, 1:2], in_=warm[:, 0:1], func=ACT.Copy)
 
         wa_raw = load_fp8(nc.sync, "wa_raw", wa_words)
-        xt_w = load_fp4(nc.sync, "xt_w", xt_words)
-        for q in range(QUADS):
-            load_scale_rows(nc.scalar, wa_s_raw, wa_scales, q)
-        nc.scalar.activation(out=warm[:, 1:2], in_=warm[:, 0:1], func=ACT.Copy)
-        for q in range(QUADS):
-            load_scale_rows(nc.sync, xt_s, xt_scales, q)
-        for q in range(QUADS):
-            load_scale_rows(nc.gpsimd, w2_s_raw, wd_scales, q, first_row=4)
         wc_raw = load_fp8(nc.sync, "wc_raw", wc_words)
+        xt_w = load_fp4(nc.sync, "xt_w", xt_words)
         xq_w = load_fp4(nc.sync, "xq_w", xq_words)
-        for q in range(QUADS):
-            load_scale_rows(nc.sync, wc_s_raw, wc_scales, q)
-        for q in range(QUADS):
-            load_scale_rows(nc.sync, xq_s, xq_scales, q)
+        for plane, scales in ((wa_s_raw, wa_scales), (xt_s, xt_scales), (wc_s_raw, wc_scales)):
+            for q in range(QUADS):
+                load_scale_rows(nc.sync, plane, scales, q)
         factor = tile("factor", [P, 2, 8], F32)
         for h, vec in enumerate((us, ur)):
             nc.sync.dma_start(out=factor[:, h, 0:PACK], in_=vec.rearrange("(p j) o -> p (j o)", j=PACK))
         wb_raw = load_fp4(nc.sync, "wb_raw", wb_words)
         wd_raw = load_fp8(nc.sync, "wd_raw", wd_words)
-        for q in range(QUADS):
-            load_scale_rows(nc.sync, w2_s_raw, wb_scales, q)
+        for first_row, scales in ((0, wb_scales), (4, wd_scales)):
+            for q in range(QUADS):
+                load_scale_rows(nc.sync, w2_s_raw, scales, q, first_row)
 
-        wa_s = deal("wa_s", wa_s_raw, U8)
         wa_w = deal("wa_w", wa_raw, I32)
         wc_w = deal("wc_w", wc_raw, I32)
+        wa_s = deal("wa_s", wa_s_raw, U8)
         wc_s = deal("wc_s", wc_s_raw, U8)
 
         upper = tile("upper", [P, 2, PACK], F32)
@@ -116,8 +112,8 @@ def tile_mix_hidden_kept_and_cut_off_pl_kernel(
         nc.scalar.activation(out=upper[:], in_=factor[:, :, 0:PACK], func=ACT.Abs)
         nc.scalar.activation(out=lower[:], in_=upper[:], func=ACT.Copy, scale=-1.0)
 
-        z = [ps.tile([P, PACK, TC], F32, name="z%d" % c) for c in range(CHUNKS)]
-        y = [ps.tile([P, PACK, TC], F32, name="y%d" % c) for c in range(CHUNKS)]
+        z = [ps.tile([P, PACK, TC], F32, name="z%d" % c, tag="z%d" % c) for c in range(CHUNKS)]
+        y = [ps.tile([P, PACK, TC], F32, name="y%d" % c) for c in range(CHUNKS - 1)]
         first = [(wa_w, wa_s, xt_w, xt_s, 0), (wa_w, wa_s, xt_w, xt_s, 1), (wc_w, wc_s, xq_w, xq_s, 0)]
         for c in range(CHUNKS):
             for n, (w, w_s, x, x_s, g) in enumerate(first):
@@ -150,23 +146,26 @@ def tile_mix_hidden_kept_and_cut_off_pl_kernel(
                         out=scaled[c][:, h, j, :], in_=z[c][:, j, :], func=ACT.Copy, scale=factor[:, h, j : j + 1]
                     )
 
-        def clip(c):
-            for h, kept in enumerate((kept_a, kept_b)):
-                for j in range(PACK):
-                    nc.vector.tensor_scalar(
-                        out=kept[c][:, j, :], in0=scaled[c][:, h, j, :],
-                        scalar1=upper[:, h, j : j + 1], scalar2=lower[:, h, j : j + 1],
-                        op0=ALU.min, op1=ALU.max,
-                    )
+        def clip(c, h):
+            kept = (kept_a, kept_b)[h]
+            for j in range(PACK):
+                nc.vector.tensor_scalar(
+                    out=kept[c][:, j, :], in0=scaled[c][:, h, j, :],
+                    scalar1=upper[:, h, j : j + 1], scalar2=lower[:, h, j : j + 1],
+                    op0=ALU.min, op1=ALU.max,
+                )
 
-        def by_word(region):
-            return region.rearrange("p j (u i) -> p u j i", i=RUN)
+        def from_regions(regions, run):
+            return regions.rearrange("p j (u i) -> p u j i", i=run)
+
+        def to_words(flat, run):
+            return flat.rearrange("p (u i j) -> p u j i", i=run, j=PACK)
 
         def interleave(c):
-            for_quant = [h16[c][:, h, :].rearrange("p (u i j) -> p u j i", i=RUN, j=PACK) for h in range(2)]
-            nc.vector.tensor_copy(out=for_quant[0], in_=by_word(kept_a[c][:]))
+            nc.vector.tensor_copy(out=to_words(h16[c][:, 0, :], 4), in_=from_regions(kept_a[c][:], 4))
             nc.vector.tensor_tensor(
-                out=for_quant[1], in0=by_word(scaled[c][:, 1]), in1=by_word(kept_b[c][:]), op=ALU.subtract
+                out=to_words(h16[c][:, 1, :], 2), in0=from_regions(scaled[c][:, 1], 2),
+                in1=from_regions(kept_b[c][:], 2), op=ALU.subtract,
             )
 
         def quantise_h(c):
@@ -174,17 +173,17 @@ def tile_mix_hidden_kept_and_cut_off_pl_kernel(
                 out=h_w[c][:].bitcast(FP8X4), scales=h_s[c][:], in_=h16[c][:].rearrange("p h w -> p (h w)")
             )
 
-        def second_layer(c, wb_w, wd_w, w2_s):
+        def second_layer(c, outs, wb_w, wd_w, w2_s):
             for i in range(PACK):
                 nc.tensor.matmul_mx(
-                    out=y[c][:, i, :],
+                    out=outs[i],
                     lhsT=wb_w[:, 0, 2 * P * i : 2 * P * (i + 1)].bitcast(FP4X4),
                     lhsT_scale=w2_s[:, 0, P * i : P * (i + 1)],
                     rhs=h_w[c][:, 0:TC].bitcast(FP8X4), rhs_scale=h_s[c][:, 0:TC],
                     start=True, stop=False,
                 )
                 nc.tensor.matmul_mx(
-                    out=y[c][:, i, :],
+                    out=outs[i],
                     lhsT=wd_w[:, 0, P * i : P * (i + 1)].bitcast(FP8X4),
                     lhsT_scale=w2_s[4:P, 0, P * i : P * (i + 1)],
                     rhs=h_w[c][:, TC : 2 * TC].bitcast(FP8X4), rhs_scale=h_s[c][:, TC : 2 * TC],
@@ -206,23 +205,40 @@ def tile_mix_hidden_kept_and_cut_off_pl_kernel(
             )
             nc.sync.dma_start(out=out_words[:, TC * c : TC * (c + 1)], in_=y_w[c][:])
 
-        for c in range(CHUNKS):
+        def whole_bank(c):
+            return [y[c][:, i, :] for i in range(PACK)]
+
+        last = CHUNKS - 1
+        for c in range(last):
             scale_z(c)
-        clip(0)
-        interleave(0)
+        clip(0, 0)
         wb_w = deal("wb_w", wb_raw, U8)
+        clip(0, 1)
+        interleave(0)
         wd_w = deal("wd_w", wd_raw, I32)
-        quantise_h(0)
         w2_s = deal("w2_s", w2_s_raw, U8)
-        second_layer(0, wb_w, wd_w, w2_s)
-        drain_y(0)
         for c in range(1, CHUNKS):
-            clip(c)
+            quantise_h(c - 1)
+            second_layer(c - 1, whole_bank(c - 1), wb_w, wd_w, w2_s)
+            drain_y(c - 1)
+            if c == 1:
+                scale_z(last)
+            clip(c, 0)
+            clip(c, 1)
             interleave(c)
-            quantise_y(c - 1)
-            quantise_h(c)
-            second_layer(c, wb_w, wd_w, w2_s)
-            drain_y(c)
+            if c > 1:
+                quantise_y(c - 2)
+        quantise_h(last)
+        quantise_y(last - 1)
+        halves = [ps.tile([P, 2, TC], F32, name="y_last%d" % e, tag="z%d" % e) for e in range(2)]
+        second_layer(last, [halves[i // 2][:, i % 2, :] for i in range(PACK)], wb_w, wd_w, w2_s)
+        nc.scalar.copy(out=y32[last][:, 0:2, :], in_=halves[0][:])
+        nc.scalar.dma_start(out=out_rows[:, 0:2, TC * last :], in_=y32[last][:, 0:2, :])
+        nc.vector.tensor_copy(out=y32[last][:, 2:4, :], in_=halves[1][:])
+        nc.sync.dma_start(out=out_rows[:, 2:4, TC * last :], in_=y32[last][:, 2:4, :])
+        nc.vector.tensor_copy(
+            out=to_words(y16[last][:].rearrange("p t i -> p (t i)"), 2), in_=from_regions(y32[last][:], 2)
+        )
         quantise_y(CHUNKS - 1)
         for q in range(QUADS):
             queue = nc.sync if q % 2 == 0 else nc.scalar

@@ -75,57 +75,80 @@ def tile_mix_hidden_kept_and_cut_off_pl_kernel(
                 )
             return dealt
 
-        xq_s = zeroed_plane("xq_s", 1, nc.gpsimd)
-        for q in range(QUADS):
-            load_scale_rows(nc.gpsimd, xq_s, xq_scales, q)
+        wc_s_raw = zeroed_plane("wc_s_raw", 1, nc.gpsimd)
+        for q in range(QUADS - 1):
+            load_scale_rows(nc.gpsimd, wc_s_raw, wc_scales, q)
+        factor = tile("factor", [P, 2, 8], F32)
+
+        def load_factor(queue, h, vec):
+            queue.dma_start(out=factor[:, h, 0:PACK], in_=vec.rearrange("(p j) o -> p (j o)", j=PACK))
+
+        load_factor(nc.gpsimd, 1, ur)
         wa_s_raw = zeroed_plane("wa_s_raw", 2)
         xt_s = zeroed_plane("xt_s", 2)
-        wc_s_raw = zeroed_plane("wc_s_raw", 1)
+        xq_s = zeroed_plane("xq_s", 1)
         w2_s_raw = zeroed_plane("w2_s_raw", 1)
         warm = tile("warm", [P, 2], F32)
         nc.vector.memset(warm[:, 0:1], 0.0)
         nc.scalar.activation(out=warm[:, 1:2], in_=warm[:, 0:1], func=ACT.Copy)
 
-        wa_raw = load_fp8(nc.sync, "wa_raw", wa_words)
         wc_raw = load_fp8(nc.sync, "wc_raw", wc_words)
-        xt_w = load_fp4(nc.sync, "xt_w", xt_words)
+        wa_raw = load_fp8(nc.sync, "wa_raw", wa_words)
         xq_w = load_fp4(nc.sync, "xq_w", xq_words)
-        for plane, scales in ((wa_s_raw, wa_scales), (xt_s, xt_scales), (wc_s_raw, wc_scales)):
+        xt_w = load_fp4(nc.sync, "xt_w", xt_words)
+        for q in range(QUADS):
+            load_scale_rows(nc.sync, wa_s_raw, wa_scales, q)
+        load_scale_rows(nc.sync, wc_s_raw, wc_scales, QUADS - 1)
+        for plane, scales in ((xt_s, xt_scales), (xq_s, xq_scales)):
             for q in range(QUADS):
                 load_scale_rows(nc.sync, plane, scales, q)
-        factor = tile("factor", [P, 2, 8], F32)
-        for h, vec in enumerate((us, ur)):
-            nc.sync.dma_start(out=factor[:, h, 0:PACK], in_=vec.rearrange("(p j) o -> p (j o)", j=PACK))
+        load_factor(nc.sync, 0, us)
         wb_raw = load_fp4(nc.sync, "wb_raw", wb_words)
         wd_raw = load_fp8(nc.sync, "wd_raw", wd_words)
         for first_row, scales in ((0, wb_scales), (4, wd_scales)):
             for q in range(QUADS):
                 load_scale_rows(nc.sync, w2_s_raw, scales, q, first_row)
 
-        wa_w = deal("wa_w", wa_raw, I32)
         wc_w = deal("wc_w", wc_raw, I32)
+        wa_w = deal("wa_w", wa_raw, I32)
         wa_s = deal("wa_s", wa_s_raw, U8)
         wc_s = deal("wc_s", wc_s_raw, U8)
 
         upper = tile("upper", [P, 2, PACK], F32)
         lower = tile("lower", [P, 2, PACK], F32)
-        nc.scalar.activation(out=upper[:], in_=factor[:, :, 0:PACK], func=ACT.Abs)
-        nc.scalar.activation(out=lower[:], in_=upper[:], func=ACT.Copy, scale=-1.0)
 
-        z = [ps.tile([P, PACK, TC], F32, name="z%d" % c, tag="z%d" % c) for c in range(CHUNKS)]
-        y = [ps.tile([P, PACK, TC], F32, name="y%d" % c) for c in range(CHUNKS - 1)]
+        def bounds(h):
+            for bound, pick in ((upper, ALU.max), (lower, ALU.min)):
+                nc.vector.scalar_tensor_tensor(
+                    out=bound[:, h, :], in0=factor[:, h, 0:PACK], scalar=-1.0, in1=factor[:, h, 0:PACK],
+                    op0=ALU.mult, op1=pick,
+                )
+
+        bounds(0)
+        bounds(1)
+
+        z0 = [ps.tile([P, 2, TC], F32, name="z0_%d" % e, tag="half%d" % e) for e in range(2)]
+        z = [z0] + [[ps.tile([P, PACK, TC], F32, name="z%d" % c)] for c in range(1, CHUNKS)]
+        y = [[ps.tile([P, PACK, TC], F32, name="y%d" % c)] for c in range(CHUNKS - 1)]
+
+        def region(banks, j):
+            per_bank = PACK // len(banks)
+            return banks[j // per_bank][:, j % per_bank, :]
+
         first = [(wa_w, wa_s, xt_w, xt_s, 0), (wa_w, wa_s, xt_w, xt_s, 1), (wc_w, wc_s, xq_w, xq_s, 0)]
         for c in range(CHUNKS):
-            for n, (w, w_s, x, x_s, g) in enumerate(first):
-                for j in range(PACK):
+            per_bank = PACK // len(z[c])
+            for j0 in range(0, PACK, per_bank):
+                passes = [(op, j) for op in first for j in range(j0, j0 + per_bank)]
+                for k, ((w, w_s, x, x_s, g), j) in enumerate(passes):
                     nc.tensor.matmul_mx(
-                        out=z[c][:, j, :],
+                        out=region(z[c], j),
                         lhsT=w[:, g, P * j : P * (j + 1)].bitcast(FP8X4),
                         lhsT_scale=w_s[:, g, P * j : P * (j + 1)],
                         rhs=x[:, g, 2 * TC * c : 2 * TC * (c + 1)].bitcast(FP4X4),
                         rhs_scale=x_s[:, g, TC * c : TC * (c + 1)],
-                        start=(n == 0 and j == 0),
-                        stop=(n == len(first) - 1 and j == PACK - 1),
+                        start=(k == 0),
+                        stop=(k == len(passes) - 1),
                     )
 
         scaled = [tile("scaled%d" % c, [P, 2, PACK, TC], F32) for c in range(CHUNKS)]
@@ -136,19 +159,18 @@ def tile_mix_hidden_kept_and_cut_off_pl_kernel(
         h_s = [tile("h_s%d" % c, [P, 2 * TC], U8) for c in range(CHUNKS)]
         y16 = [tile("y16_%d" % c, [P, TC, PACK], BF16) for c in range(CHUNKS)]
         y32 = [tile("y32_%d" % c, [P, PACK, TC], F32) for c in range(CHUNKS)]
-        y_w = [tile("y_w%d" % c, [P, TC], I32) for c in range(CHUNKS)]
+        y_w = tile("y_w", [P, T], I32)
         y_s = tile("y_s", [P, T], U8)
 
-        def scale_z(c):
-            for h in range(2):
-                for j in range(PACK):
-                    nc.scalar.activation(
-                        out=scaled[c][:, h, j, :], in_=z[c][:, j, :], func=ACT.Copy, scale=factor[:, h, j : j + 1]
-                    )
+        def scale_z(c, h, regions=range(PACK)):
+            for j in regions:
+                nc.scalar.activation(
+                    out=scaled[c][:, h, j, :], in_=region(z[c], j), func=ACT.Copy, scale=factor[:, h, j : j + 1]
+                )
 
-        def clip(c, h):
+        def clip(c, h, regions=range(PACK)):
             kept = (kept_a, kept_b)[h]
-            for j in range(PACK):
+            for j in regions:
                 nc.vector.tensor_scalar(
                     out=kept[c][:, j, :], in0=scaled[c][:, h, j, :],
                     scalar1=upper[:, h, j : j + 1], scalar2=lower[:, h, j : j + 1],
@@ -161,85 +183,106 @@ def tile_mix_hidden_kept_and_cut_off_pl_kernel(
         def to_words(flat, run):
             return flat.rearrange("p (u i j) -> p u j i", i=run, j=PACK)
 
-        def interleave(c):
+        def interleave_a(c):
             nc.vector.tensor_copy(out=to_words(h16[c][:, 0, :], 4), in_=from_regions(kept_a[c][:], 4))
+
+        def interleave_b(c):
             nc.vector.tensor_tensor(
                 out=to_words(h16[c][:, 1, :], 2), in0=from_regions(scaled[c][:, 1], 2),
                 in1=from_regions(kept_b[c][:], 2), op=ALU.subtract,
             )
 
-        def quantise_h(c):
+        def quantise_h(c, h0, h1):
             nc.vector.quantize_mx(
-                out=h_w[c][:].bitcast(FP8X4), scales=h_s[c][:], in_=h16[c][:].rearrange("p h w -> p (h w)")
+                out=h_w[c][:, TC * h0 : TC * h1].bitcast(FP8X4), scales=h_s[c][:, TC * h0 : TC * h1],
+                in_=h16[c][:, h0:h1, :].rearrange("p h w -> p (h w)"),
             )
 
-        def second_layer(c, outs, wb_w, wd_w, w2_s):
+        def second_layer(c, outs, h):
+            per_bank = PACK // len(outs)
             for i in range(PACK):
+                if h == 0:
+                    weights = wb_w[:, 0, 2 * P * i : 2 * P * (i + 1)].bitcast(FP4X4)
+                else:
+                    weights = wd_w[:, 0, P * i : P * (i + 1)].bitcast(FP8X4)
                 nc.tensor.matmul_mx(
-                    out=outs[i],
-                    lhsT=wb_w[:, 0, 2 * P * i : 2 * P * (i + 1)].bitcast(FP4X4),
-                    lhsT_scale=w2_s[:, 0, P * i : P * (i + 1)],
-                    rhs=h_w[c][:, 0:TC].bitcast(FP8X4), rhs_scale=h_s[c][:, 0:TC],
-                    start=True, stop=False,
-                )
-                nc.tensor.matmul_mx(
-                    out=outs[i],
-                    lhsT=wd_w[:, 0, P * i : P * (i + 1)].bitcast(FP8X4),
-                    lhsT_scale=w2_s[4:P, 0, P * i : P * (i + 1)],
-                    rhs=h_w[c][:, TC : 2 * TC].bitcast(FP8X4), rhs_scale=h_s[c][:, TC : 2 * TC],
-                    start=False, stop=True,
+                    out=region(outs, i),
+                    lhsT=weights,
+                    lhsT_scale=w2_s[4 * h : P, 0, P * i : P * (i + 1)],
+                    rhs=h_w[c][:, TC * h : TC * (h + 1)].bitcast(FP8X4), rhs_scale=h_s[c][:, TC * h : TC * (h + 1)],
+                    start=(h == 0 and i % per_bank == 0), stop=(h == 1 and i % per_bank == per_bank - 1),
                 )
 
         out_rows = out_0.rearrange("(p i) t -> p i t", i=PACK)
         out_words = out_1.rearrange("z p c b -> p (z c b)").bitcast(I32)
 
         def drain_y(c):
-            nc.scalar.copy(out=y16[c][:], in_=y[c][:].rearrange("p i t -> p t i"))
-            nc.scalar.copy(out=y32[c][:], in_=y[c][:])
+            if c < CHUNKS - 2:
+                nc.scalar.copy(out=y16[c][:], in_=y[c][0][:].rearrange("p i t -> p t i"))
+            nc.scalar.copy(out=y32[c][:], in_=y[c][0][:])
             nc.sync.dma_start(out=out_rows[:, :, TC * c : TC * (c + 1)], in_=y32[c][:])
+
+        def round_y(c):
+            nc.vector.tensor_copy(
+                out=to_words(y16[c][:].rearrange("p t i -> p (t i)"), 2), in_=from_regions(y32[c][:], 2)
+            )
 
         def quantise_y(c):
             nc.vector.quantize_mx(
-                out=y_w[c][:].bitcast(FP8X4), scales=y_s[:, TC * c : TC * (c + 1)],
+                out=y_w[:, TC * c : TC * (c + 1)].bitcast(FP8X4), scales=y_s[:, TC * c : TC * (c + 1)],
                 in_=y16[c][:].rearrange("p t i -> p (t i)"),
             )
-            nc.sync.dma_start(out=out_words[:, TC * c : TC * (c + 1)], in_=y_w[c][:])
 
-        def whole_bank(c):
-            return [y[c][:, i, :] for i in range(PACK)]
+        def finish(c):
+            quantise_h(c, 0, 2)
+            second_layer(c, y[c], 0)
+            second_layer(c, y[c], 1)
+            drain_y(c)
 
         last = CHUNKS - 1
-        for c in range(last):
-            scale_z(c)
-        clip(0, 0)
+        for pair in ((0, 1), (2, 3)):
+            for h in range(2):
+                scale_z(0, h, pair)
+        for c in range(1, CHUNKS):
+            for h in range(2):
+                scale_z(c, h)
+        clip(0, 0, (0, 1))
+        clip(0, 1, (0, 1))
         wb_w = deal("wb_w", wb_raw, U8)
-        clip(0, 1)
-        interleave(0)
+        clip(0, 0, (2, 3))
+        clip(0, 1, (2, 3))
+        interleave_a(0)
+        interleave_b(0)
         wd_w = deal("wd_w", wd_raw, I32)
         w2_s = deal("w2_s", w2_s_raw, U8)
-        for c in range(1, CHUNKS):
-            quantise_h(c - 1)
-            second_layer(c - 1, whole_bank(c - 1), wb_w, wd_w, w2_s)
-            drain_y(c - 1)
-            if c == 1:
-                scale_z(last)
+        for c in range(1, last):
             clip(c, 0)
+            finish(c - 1)
             clip(c, 1)
-            interleave(c)
-            if c > 1:
-                quantise_y(c - 2)
-        quantise_h(last)
-        quantise_y(last - 1)
-        halves = [ps.tile([P, 2, TC], F32, name="y_last%d" % e, tag="z%d" % e) for e in range(2)]
-        second_layer(last, [halves[i // 2][:, i % 2, :] for i in range(PACK)], wb_w, wd_w, w2_s)
+            interleave_a(c)
+            interleave_b(c)
+        clip(last, 0)
+        finish(last - 1)
+        interleave_a(last)
+        clip(last, 1)
+        halves = [ps.tile([P, 2, TC], F32, name="y_last%d" % e, tag="half%d" % e) for e in range(2)]
+        quantise_h(last, 0, 1)
+        second_layer(last, halves, 0)
+        interleave_b(last)
+        quantise_y(0)
+        quantise_h(last, 1, 2)
+        second_layer(last, halves, 1)
+        quantise_y(1)
+        nc.sync.dma_start(out=out_words[:, : 2 * TC], in_=y_w[:, : 2 * TC])
+        round_y(2)
         nc.scalar.copy(out=y32[last][:, 0:2, :], in_=halves[0][:])
         nc.scalar.dma_start(out=out_rows[:, 0:2, TC * last :], in_=y32[last][:, 0:2, :])
         nc.vector.tensor_copy(out=y32[last][:, 2:4, :], in_=halves[1][:])
         nc.sync.dma_start(out=out_rows[:, 2:4, TC * last :], in_=y32[last][:, 2:4, :])
-        nc.vector.tensor_copy(
-            out=to_words(y16[last][:].rearrange("p t i -> p (t i)"), 2), in_=from_regions(y32[last][:], 2)
-        )
-        quantise_y(CHUNKS - 1)
+        quantise_y(2)
+        round_y(last)
+        quantise_y(last)
+        nc.sync.dma_start(out=out_words[:, 2 * TC :], in_=y_w[:, 2 * TC :])
         for q in range(QUADS):
             queue = nc.sync if q % 2 == 0 else nc.scalar
             queue.dma_start(

@@ -126,6 +126,8 @@ def tile_mix_hidden_kept_and_cut_off_pl_kernel(
 
         bounds(0)
         bounds(1)
+        minus_ur = tile("minus_ur", [P, PACK], F32)
+        nc.vector.tensor_scalar(out=minus_ur[:], in0=factor[:, 1, 0:PACK], scalar1=-1.0, scalar2=None, op0=ALU.mult)
 
         z0 = [ps.tile([P, 2, TC], F32, name="z0_%d" % e, tag="half%d" % e) for e in range(2)]
         z = [z0] + [[ps.tile([P, PACK, TC], F32, name="z%d" % c)] for c in range(1, CHUNKS)]
@@ -167,6 +169,14 @@ def tile_mix_hidden_kept_and_cut_off_pl_kernel(
                 nc.scalar.activation(
                     out=scaled[c][:, h, j, :], in_=region(z[c], j), func=ACT.Copy, scale=factor[:, h, j : j + 1]
                 )
+
+        def cut_off_sides(c):
+            for j in range(PACK):
+                for side, slope in ((scaled[c][:, 1], factor[:, 1, :]), (kept_b[c], minus_ur)):
+                    nc.scalar.activation(
+                        out=side[:, j, :], in_=region(z[c], j), func=ACT.Relu,
+                        scale=slope[:, j : j + 1], bias=lower[:, 1, j : j + 1],
+                    )
 
         def clip(c, h, regions=range(PACK)):
             kept = (kept_a, kept_b)[h]
@@ -244,8 +254,11 @@ def tile_mix_hidden_kept_and_cut_off_pl_kernel(
             for h in range(2):
                 scale_z(0, h, pair)
         for c in range(1, CHUNKS):
-            for h in range(2):
-                scale_z(c, h)
+            scale_z(c, 0)
+            if c == 2:
+                cut_off_sides(c)
+            else:
+                scale_z(c, 1)
         clip(0, 0, (0, 1))
         clip(0, 1, (0, 1))
         wb_w = deal("wb_w", wb_raw, U8)
@@ -258,7 +271,8 @@ def tile_mix_hidden_kept_and_cut_off_pl_kernel(
         for c in range(1, last):
             clip(c, 0)
             finish(c - 1)
-            clip(c, 1)
+            if c != 2:
+                clip(c, 1)
             interleave_a(c)
             interleave_b(c)
         clip(last, 0)
@@ -276,16 +290,14 @@ def tile_mix_hidden_kept_and_cut_off_pl_kernel(
         nc.sync.dma_start(out=out_words[:, : 2 * TC], in_=y_w[:, : 2 * TC])
         round_y(2)
         nc.scalar.copy(out=y32[last][:, 0:2, :], in_=halves[0][:])
-        nc.scalar.dma_start(out=out_rows[:, 0:2, TC * last :], in_=y32[last][:, 0:2, :])
         nc.vector.tensor_copy(out=y32[last][:, 2:4, :], in_=halves[1][:])
-        nc.sync.dma_start(out=out_rows[:, 2:4, TC * last :], in_=y32[last][:, 2:4, :])
+        nc.sync.dma_start(out=out_rows[:, :, TC * last :], in_=y32[last][:])
         quantise_y(2)
         round_y(last)
         quantise_y(last)
         nc.sync.dma_start(out=out_words[:, 2 * TC :], in_=y_w[:, 2 * TC :])
         for q in range(QUADS):
-            queue = nc.sync if q % 2 == 0 else nc.scalar
-            queue.dma_start(
+            nc.scalar.dma_start(
                 out=out_2[0, 4 * q : 4 * q + 4, :].bitcast(I32),
                 in_=y_s[:].bitcast(I32)[32 * q : 32 * q + 4],
             )

from contextlib import ExitStack

import concourse.mybir as mybir

K, L, T, R, N = 1024, 512, 512, 512, 512
FLOPS = 2 * T * (K * R + L * R + 2 * R * N)

F32 = mybir.dt.float32
BF16 = mybir.dt.bfloat16
I32 = mybir.dt.int32
U8 = mybir.dt.uint8
FP8X4 = mybir.dt.float8_e4m3fn_x4
FP4X4 = mybir.dt.float4_e2m1fn_x4
ALU = mybir.AluOpType
ACT = mybir.ActivationFunctionType

P = 128
PACK = 4
QUADS = 4
TC = 128
CHUNKS = T // TC


def tile_mix_hidden_kept_and_cut_off_pl_kernel(
    tc, xt_words, xt_scales, wa_words, wa_scales, xq_words, xq_scales, wc_words, wc_scales,
    us, ur, wb_words, wb_scales, wd_words, wd_scales, out_0, out_1, out_2,
):
    nc = tc.nc
    with ExitStack() as ctx:
        sb = ctx.enter_context(tc.tile_pool(name="sb", bufs=1))
        ps = ctx.enter_context(tc.psum_pool(name="ps", bufs=1))
        ctx.enter_context(tc.manual_schedule())

        def tile(name, shape, dtype):
            return sb.tile(shape, dtype, name=name, align_bytes=64)

        def load_fp8(queue, name, words):
            passes = words.shape[0]
            raw = tile(name, [P, passes, words.shape[2]], I32)
            queue.dma_start(out=raw[:], in_=words.rearrange("z p c b -> p z (c b)").bitcast(I32))
            return raw

        def load_fp4(queue, name, words):
            passes = words.shape[0]
            raw = tile(name, [P, passes, words.shape[2]], U8)
            queue.dma_start(out=raw[:].bitcast(I32), in_=words.rearrange("z p c -> p z c").bitcast(I32))
            return raw

        def zeroed_plane(name, passes, engine=nc.vector):
            plane = tile(name, [P, passes, T], U8)
            engine.memset(plane[:].bitcast(I32), 0)
            return plane

        def load_scale_rows(queue, plane, scales, quad, first_row=0):
            lo = 32 * quad + first_row
            queue.dma_start(
                out=plane[:].bitcast(I32)[lo : lo + 4],
                in_=scales[:, 4 * quad : 4 * quad + 4, :].rearrange("z r c -> r z c").bitcast(I32),
            )

        def deal(name, raw, dtype):
            passes, width = raw.shape[1], raw.shape[2]
            dealt = tile(name, [P, passes, width], dtype)
            b = width // (PACK * P)
            if b == 1:
                pair = 2 if dtype == I32 else P
                nc.vector.tensor_copy(
                    out=dealt[:].rearrange("p z (j u i) -> p z u j i", j=PACK, i=pair),
                    in_=raw[:].rearrange("p z (u i j) -> p z u j i", j=PACK, i=pair),
                )
            else:
                nc.vector.tensor_copy(
                    out=dealt[:, 0, :].rearrange("p (j m b) -> p j m b", j=PACK, b=b),
                    in_=raw[:, 0, :].rearrange("p (m j b) -> p j m b", j=PACK, b=b),
                )
            return dealt

        wc_s_raw = zeroed_plane("wc_s_raw", 1, nc.gpsimd)
        for q in range(QUADS - 1):
            load_scale_rows(nc.gpsimd, wc_s_raw, wc_scales, q)
        factor = tile("factor", [P, 2, 8], F32)

        def load_factor(queue, h, vec):
            queue.dma_start(out=factor[:, h, 0:PACK], in_=vec.rearrange("(p j) o -> p (j o)", j=PACK))

        load_factor(nc.gpsimd, 1, ur)
        wa_s_raw = zeroed_plane("wa_s_raw", 2)
        xt_s = zeroed_plane("xt_s", 2)
        xq_s = zeroed_plane("xq_s", 1)
        w2_s_raw = zeroed_plane("w2_s_raw", 1)
        warm = tile("warm", [P, 2], F32)
        nc.vector.memset(warm[:, 0:1], 0.0)
        nc.scalar.activation(out=warm[:, 1:2], in_=warm[:, 0:1], func=ACT.Copy)

        wc_raw = load_fp8(nc.sync, "wc_raw", wc_words)
        wa_raw = load_fp8(nc.sync, "wa_raw", wa_words)
        xq_w = load_fp4(nc.sync, "xq_w", xq_words)
        xt_w = load_fp4(nc.sync, "xt_w", xt_words)
        for q in range(QUADS):
            load_scale_rows(nc.sync, wa_s_raw, wa_scales, q)
        load_scale_rows(nc.sync, wc_s_raw, wc_scales, QUADS - 1)
        for plane, scales in ((xt_s, xt_scales), (xq_s, xq_scales)):
            for q in range(QUADS):
                load_scale_rows(nc.sync, plane, scales, q)
        load_factor(nc.sync, 0, us)
        wb_raw = load_fp4(nc.sync, "wb_raw", wb_words)
        wd_raw = load_fp8(nc.sync, "wd_raw", wd_words)
        for first_row, scales in ((0, wb_scales), (4, wd_scales)):
            for q in range(QUADS):
                load_scale_rows(nc.sync, w2_s_raw, scales, q, first_row)

        wc_w = deal("wc_w", wc_raw, I32)
        wa_w = deal("wa_w", wa_raw, I32)
        wa_s = deal("wa_s", wa_s_raw, U8)
        wc_s = deal("wc_s", wc_s_raw, U8)

        upper = tile("upper", [P, 2, PACK], F32)
        lower = tile("lower", [P, 2, PACK], F32)

        def bounds(h):
            for bound, pick in ((upper, ALU.max), (lower, ALU.min)):
                nc.vector.scalar_tensor_tensor(
                    out=bound[:, h, :], in0=factor[:, h, 0:PACK], scalar=-1.0, in1=factor[:, h, 0:PACK],
                    op0=ALU.mult, op1=pick,
                )

        bounds(0)
        bounds(1)
        minus_ur = tile("minus_ur", [P, PACK], F32)
        nc.vector.tensor_scalar(out=minus_ur[:], in0=factor[:, 1, 0:PACK], scalar1=-1.0, scalar2=None, op0=ALU.mult)

        z0 = [ps.tile([P, 2, TC], F32, name="z0_%d" % e, tag="half%d" % e) for e in range(2)]
        z = [z0] + [[ps.tile([P, PACK, TC], F32, name="z%d" % c)] for c in range(1, CHUNKS)]
        y = [[ps.tile([P, PACK, TC], F32, name="y%d" % c)] for c in range(CHUNKS - 1)]

        def region(banks, j):
            per_bank = PACK // len(banks)
            return banks[j // per_bank][:, j % per_bank, :]

        first = [(wa_w, wa_s, xt_w, xt_s, 0), (wa_w, wa_s, xt_w, xt_s, 1), (wc_w, wc_s, xq_w, xq_s, 0)]
        for c in range(CHUNKS):
            per_bank = PACK // len(z[c])
            for j0 in range(0, PACK, per_bank):
                passes = [(op, j) for op in first for j in range(j0, j0 + per_bank)]
                for k, ((w, w_s, x, x_s, g), j) in enumerate(passes):
                    nc.tensor.matmul_mx(
                        out=region(z[c], j),
                        lhsT=w[:, g, P * j : P * (j + 1)].bitcast(FP8X4),
                        lhsT_scale=w_s[:, g, P * j : P * (j + 1)],
                        rhs=x[:, g, 2 * TC * c : 2 * TC * (c + 1)].bitcast(FP4X4),
                        rhs_scale=x_s[:, g, TC * c : TC * (c + 1)],
                        start=(k == 0),
                        stop=(k == len(passes) - 1),
                    )

        scaled = [tile("scaled%d" % c, [P, 2, PACK, TC], F32) for c in range(CHUNKS)]
        kept_a = [tile("kept_a%d" % c, [P, PACK, TC], BF16) for c in range(CHUNKS)]
        kept_b = [tile("kept_b%d" % c, [P, PACK, TC], F32) for c in range(CHUNKS)]
        h16 = [tile("h16_%d" % c, [P, 2, TC * PACK], BF16) for c in range(CHUNKS)]
        h_w = [tile("h_w%d" % c, [P, 2 * TC], I32) for c in range(CHUNKS)]
        h_s = [tile("h_s%d" % c, [P, 2 * TC], U8) for c in range(CHUNKS)]
        y16 = [tile("y16_%d" % c, [P, TC, PACK], BF16) for c in range(CHUNKS)]
        y32 = [tile("y32_%d" % c, [P, PACK, TC], F32) for c in range(CHUNKS)]
        y_w = tile("y_w", [P, T], I32)
        y_s = tile("y_s", [P, T], U8)

        def scale_z(c, h, regions=range(PACK)):
            for j in regions:
                nc.scalar.activation(
                    out=scaled[c][:, h, j, :], in_=region(z[c], j), func=ACT.Copy, scale=factor[:, h, j : j + 1]
                )

        def cut_off_sides(c):
            for j in range(PACK):
                for side, slope in ((scaled[c][:, 1], factor[:, 1, :]), (kept_b[c], minus_ur)):
                    nc.scalar.activation(
                        out=side[:, j, :], in_=region(z[c], j), func=ACT.Relu,
                        scale=slope[:, j : j + 1], bias=lower[:, 1, j : j + 1],
                    )

        def clip(c, h, regions=range(PACK)):
            kept = (kept_a, kept_b)[h]
            for j in regions:
                nc.vector.tensor_scalar(
                    out=kept[c][:, j, :], in0=scaled[c][:, h, j, :],
                    scalar1=upper[:, h, j : j + 1], scalar2=lower[:, h, j : j + 1],
                    op0=ALU.min, op1=ALU.max,
                )

        def from_regions(regions, run):
            return regions.rearrange("p j (u i) -> p u j i", i=run)

        def to_words(flat, run):
            return flat.rearrange("p (u i j) -> p u j i", i=run, j=PACK)

        def interleave_a(c):
            nc.vector.tensor_copy(out=to_words(h16[c][:, 0, :], 4), in_=from_regions(kept_a[c][:], 4))

        def interleave_b(c):
            nc.vector.tensor_tensor(
                out=to_words(h16[c][:, 1, :], 2), in0=from_regions(scaled[c][:, 1], 2),
                in1=from_regions(kept_b[c][:], 2), op=ALU.subtract,
            )

        def quantise_h(c, h0, h1):
            nc.vector.quantize_mx(
                out=h_w[c][:, TC * h0 : TC * h1].bitcast(FP8X4), scales=h_s[c][:, TC * h0 : TC * h1],
                in_=h16[c][:, h0:h1, :].rearrange("p h w -> p (h w)"),
            )

        def second_layer(c, outs, h):
            per_bank = PACK // len(outs)
            for i in range(PACK):
                if h == 0:
                    weights = wb_w[:, 0, 2 * P * i : 2 * P * (i + 1)].bitcast(FP4X4)
                else:
                    weights = wd_w[:, 0, P * i : P * (i + 1)].bitcast(FP8X4)
                nc.tensor.matmul_mx(
                    out=region(outs, i),
                    lhsT=weights,
                    lhsT_scale=w2_s[4 * h : P, 0, P * i : P * (i + 1)],
                    rhs=h_w[c][:, TC * h : TC * (h + 1)].bitcast(FP8X4), rhs_scale=h_s[c][:, TC * h : TC * (h + 1)],
                    start=(h == 0 and i % per_bank == 0), stop=(h == 1 and i % per_bank == per_bank - 1),
                )

        out_rows = out_0.rearrange("(p i) t -> p i t", i=PACK)
        out_words = out_1.rearrange("z p c b -> p (z c b)").bitcast(I32)

        def drain_y(c):
            if c < CHUNKS - 2:
                nc.scalar.copy(out=y16[c][:], in_=y[c][0][:].rearrange("p i t -> p t i"))
            nc.scalar.copy(out=y32[c][:], in_=y[c][0][:])
            nc.sync.dma_start(out=out_rows[:, :, TC * c : TC * (c + 1)], in_=y32[c][:])

        def round_y(c):
            nc.vector.tensor_copy(
                out=to_words(y16[c][:].rearrange("p t i -> p (t i)"), 2), in_=from_regions(y32[c][:], 2)
            )

        def quantise_y(c):
            nc.vector.quantize_mx(
                out=y_w[:, TC * c : TC * (c + 1)].bitcast(FP8X4), scales=y_s[:, TC * c : TC * (c + 1)],
                in_=y16[c][:].rearrange("p t i -> p (t i)"),
            )

        def finish(c):
            quantise_h(c, 0, 2)
            second_layer(c, y[c], 0)
            second_layer(c, y[c], 1)
            drain_y(c)

        last = CHUNKS - 1
        for pair in ((0, 1), (2, 3)):
            for h in range(2):
                scale_z(0, h, pair)
        for c in range(1, CHUNKS):
            scale_z(c, 0)
            if c == 2:
                cut_off_sides(c)
            else:
                scale_z(c, 1)
        clip(0, 0, (0, 1))
        clip(0, 1, (0, 1))
        wb_w = deal("wb_w", wb_raw, U8)
        clip(0, 0, (2, 3))
        clip(0, 1, (2, 3))
        interleave_a(0)
        interleave_b(0)
        wd_w = deal("wd_w", wd_raw, I32)
        w2_s = deal("w2_s", w2_s_raw, U8)
        for c in range(1, last):
            clip(c, 0)
            finish(c - 1)
            if c != 2:
                clip(c, 1)
            interleave_a(c)
            interleave_b(c)
        clip(last, 0)
        finish(last - 1)
        interleave_a(last)
        clip(last, 1)
        halves = [ps.tile([P, 2, TC], F32, name="y_last%d" % e, tag="half%d" % e) for e in range(2)]
        quantise_h(last, 0, 1)
        second_layer(last, halves, 0)
        interleave_b(last)
        quantise_y(0)
        quantise_h(last, 1, 2)
        second_layer(last, halves, 1)
        quantise_y(1)
        nc.sync.dma_start(out=out_words[:, : 2 * TC], in_=y_w[:, : 2 * TC])
        round_y(2)
        nc.scalar.copy(out=y32[last][:, 0:2, :], in_=halves[0][:])
        nc.vector.tensor_copy(out=y32[last][:, 2:4, :], in_=halves[1][:])
        nc.sync.dma_start(out=out_rows[:, :, TC * last :], in_=y32[last][:])
        quantise_y(2)
        round_y(last)
        quantise_y(last)
        nc.sync.dma_start(out=out_words[:, 2 * TC :], in_=y_w[:, 2 * TC :])
        for q in range(QUADS):
            nc.scalar.dma_start(
                out=out_2[0, 4 * q : 4 * q + 4, :].bitcast(I32),
                in_=y_s[:].bitcast(I32)[32 * q : 32 * q + 4],
            )
